import numpy as np
import ml_dtypes


def mxq(x, axis, fmt="e4m3"):
    dtype, down = {"e4m3": (ml_dtypes.float8_e4m3fn, 7), "e5m2": (ml_dtypes.float8_e5m2, 14)}[fmt]
    v = np.moveaxis(np.asarray(x, np.float32).astype(ml_dtypes.bfloat16).astype(np.float64), axis, -1)
    blocks = v.reshape(v.shape[:-1] + (-1, 32))
    amax = np.abs(blocks).max(-1, keepdims=True)
    byte = np.maximum(np.where(amax > 0, np.frexp(amax)[1] - 1 + 127, 0) - down, 1)
    scale = np.exp2(byte - 127.0)
    codes = (blocks / scale).astype(np.float32).astype(dtype).astype(np.float64)
    return np.moveaxis((codes * scale).reshape(v.shape), -1, axis)


WIDE = False


def mx_kscale(k):
    if not WIDE:
        return np.ones(k)
    levels = np.array([10, -10, 5, -5, 0])
    if k % 512:
        return np.exp2(np.random.permutation(np.resize(levels, k // 32))).repeat(32)
    a = np.empty((k // 512, 16))
    for p in range(k // 512):
        a[p, :8] = np.random.permutation(np.resize(levels, 8))
        for g in range(8):
            far = levels[np.abs(levels - a[p, g]) >= 10]
            a[p, g + 8] = far[np.random.randint(len(far))]
    return np.exp2(a.ravel()).repeat(32)


def f64(x):
    return np.asarray(x).astype(np.float64)


def striped(idx):
    return np.tile(idx.reshape(-1, 16).T, (8, 1)).astype(np.uint16)


def unstriped(offs):
    return offs[:16].T.reshape(-1).astype(np.int64)


def striped8(idx):
    return np.concatenate([x.reshape(-1, 16).T for x in idx]).astype(np.uint16)


def runs(offs, k):
    lists = np.stack([offs[16 * r : 16 * r + 16].T.reshape(-1) for r in range(8)]).astype(np.int64)
    return lists[np.arange(k) % 512 // 64]


def pack_weight(w):
    k, n = w.shape
    w = f64(np.asarray(w, np.float32).astype(ml_dtypes.bfloat16)).reshape(k // 32, 32, n)
    amax = np.abs(w).max(1)
    byte = np.clip(np.where(amax > 0, np.frexp(amax)[1] - 1 + 127 - 7, 1), 1, 254)
    scaled = (w * np.exp2(127.0 - byte)[:, None, :]).reshape(k, n).astype(np.float32)
    words = np.ascontiguousarray(scaled.reshape(k // 512, 128, 4, n).transpose(0, 1, 3, 2)).astype(ml_dtypes.float8_e4m3fn).view(np.uint8)
    return words, np.ascontiguousarray(byte.astype(np.uint8).reshape(k // 512, 16, n))


def unpack_weight(words, scales):
    g, p, n, _ = words.shape
    vals = np.ascontiguousarray(words).view(ml_dtypes.float8_e4m3fn).astype(np.float64) * np.repeat(np.exp2(scales.astype(np.float64) - 127.0), 8, axis=1)[..., None]
    return vals.transpose(0, 1, 3, 2).reshape(g * 512, n)


def sigmoid(v):
    return 1.0 / (1.0 + np.exp(-np.maximum(v, -700.0)))


K, T, S, H, C, U = 512, 2048, 256, 512, 512, 512


def setup_inputs():
    n = np.random.standard_normal
    s = mx_kscale(K)[:, None]
    packed_xT = pack_weight(n((K, T)) * s)
    perm = np.random.permutation(U)
    return {
        "x_words": packed_xT[0],
        "x_scales": packed_xT[1],
        "w1": (n((K, H)) / np.sqrt(2 * K) / s).astype(np.float32),
        "w2": (n((K, H)) / np.sqrt(2 * K) / s).astype(np.float32),
        "sl": np.random.uniform(1.0, 2.0, (H, 1)).astype(np.float32),
        "th": (0.5 * n((H, 1))).astype(np.float32),
        "gs": (np.random.uniform(0.5, 1.5, (K, 1)) / s).astype(np.float32),
        "offs": striped(np.random.permutation(T)[:S]),
        "hz": striped8(np.random.randint(0, T, (8, S))),
        "n1": striped(np.random.permutation(S)),
        "n2": striped(np.random.permutation(S)),
        "cand": striped(np.random.permutation(T)[:C]),
        "n3": striped(perm[:S]),
        "n4": striped(perm[S:]),
        "n5": striped(np.random.permutation(S)),
    }


def reference(x_words, x_scales, w1, w2, sl, th, gs, offs, hz, n1, n2, cand, n3, n4, n5):
    x_cand = unpack_weight(x_words, x_scales)[:, unstriped(cand)]
    xq = unpack_weight(x_words, x_scales)[:, unstriped(offs)]
    x_hz = unpack_weight(x_words, x_scales)[np.arange(K)[:, None], runs(hz, K)]
    y = mxq(f64(w1), 0, "e4m3").T @ xq + mxq(f64(w2), 0, "e4m3").T @ x_hz
    ds = np.zeros((H, S))
    ds[:, unstriped(n1)] = y
    sg = sigmoid(f64(sl) * (ds[:, unstriped(n2)] - f64(th)))
    z = f64(gs) * (y * sg)
    s = 0.0625 * ((x_cand.T @ mxq(z, 0, "e4m3")))
    dn = np.minimum(s, s[:, unstriped(n5)])
    up = np.maximum(s, s[:, unstriped(n5)])
    ph = np.zeros((C, U))
    ph[:, unstriped(n3)] = up
    out = ph.copy()
    out[:, unstriped(n4)] = dn
    return out

@@ -1,0 +1,242 @@
+from contextlib import ExitStack
+
+import concourse.mybir as mybir
+
+F32 = mybir.dt.float32
+BF16 = mybir.dt.bfloat16
+I32 = mybir.dt.int32
+U32 = mybir.dt.uint32
+U16 = mybir.dt.uint16
+U8 = mybir.dt.uint8
+FP8X4 = mybir.dt.float8_e4m3fn_x4
+ALU = mybir.AluOpType
+ACT = mybir.ActivationFunctionType
+
+P = 128
+K, T, S, H, C, U = 512, 2048, 256, 512, 512, 512
+FLOPS = 2 * K * H * S * 2 + 2 * K * C * S
+HALF = S // 2
+
+
+def tile_picked_thcerlpagmx_none_p_kernel(
+    tc, x_words, x_scales, w1, w2, sl, th, gs, offs, hz, n1, n2, cand, n3, n4, n5, out
+):
+    nc = tc.nc
+    with ExitStack() as ctx:
+        lists = ctx.enter_context(tc.tile_pool(name="lists", bufs=1))
+        sb = ctx.enter_context(tc.tile_pool(name="sb", bufs=1))
+        shared = ctx.enter_context(tc.tile_pool(name="shared", bufs=1))
+        ps = ctx.enter_context(tc.psum_pool(name="ps", bufs=1))
+
+        def load_list(src, name):
+            tile = lists.tile(list(src.shape), U16, name=name)
+            nc.sync.dma_start(tile[:], src)
+            return tile
+
+        def load_w(w, half, raw):
+            nc.sync.dma_start(raw[:], w.rearrange("(p j) c -> p j c", j=4)[:, :, half * (H // 2) : (half + 1) * (H // 2)])
+            return raw
+
+        scale_table = shared.tile([P, T], U8, name="scale_table", offset=3072)
+        nc.vector.memset(scale_table[:].bitcast(I32), 0)
+        for e in range(2):
+            nc.scalar.dma_start(scale_table[e:P:16, :].bitcast(I32), x_scales[0][e:16:2, :].bitcast(I32))
+
+        hz_l = load_list(hz, "hz_l")
+        offs_l = load_list(offs, "offs_l")
+        cand_l = load_list(cand, "cand_l")
+        word_table = sb.tile([P, T], U32, name="word_table", align_bytes=64)
+        nc.sync.dma_start(word_table[:].bitcast(I32), x_words[0].rearrange("p n t -> p (n t)").bitcast(I32))
+        n1_l = load_list(n1, "n1_l")
+        n2_l = load_list(n2, "n2_l")
+        raw = {}
+        raw[0, 0] = load_w(w1, 0, sb.tile([P, 4, H // 2], F32, name="raw00"))
+        raw[1, 0] = load_w(w2, 0, sb.tile([P, 4, H // 2], F32, name="raw10"))
+        n5_l = load_list(n5, "n5_l")
+        n3_l = load_list(n3, "n3_l")
+        n4_l = load_list(n4, "n4_l")
+
+        even = {}
+        rows4 = {}
+        for name, src in (("sl", sl), ("th", th), ("gs", gs)):
+            even[name] = sb.tile([P, 2], F32, name="even_" + name)
+            with nc.allow_non_contiguous_dma(reason="one value a partition"):
+                nc.gpsimd.dma_start(even[name][:], src.rearrange("(h q two) o -> q h (two o)", h=2, two=2)[:, :, 0])
+        even_bias = sb.tile([P, 2], F32, name="even_bias")
+        nc.gpsimd.tensor_tensor(even_bias[:], even["sl"][:], even["th"][:], ALU.mult)
+        nc.gpsimd.tensor_scalar(even_bias[:], even_bias[:], -1.0, None, ALU.mult)
+
+        pages = []
+        for c in range(4):
+            page = sb.tile([P, U], F32, name="page%d" % c)
+            pages.append(page)
+
+        def move_odd_rows(plane, gathered):
+            for e in range(2):
+                nc.sync.dma_start(plane[2 + e : P : 32, :].bitcast(I32), gathered[16 + e : P : 32, :].bitcast(I32))
+
+        picked_bytes = sb.tile([P, 2 * S], U8, name="picked_bytes", tag="picked_bytes", align_bytes=64)
+        nc.vector.tensor_copy(picked_bytes[:, S:], scale_table[:].indirect(hz_l[:]))
+        nc.vector.tensor_copy(picked_bytes[:, :S], scale_table[:].indirect(offs_l[:]))
+        x_plane = sb.tile([P, 2 * S], U8, name="x_plane", align_bytes=64)
+        nc.vector.memset(x_plane[:].bitcast(I32), 0)
+        move_odd_rows(x_plane, picked_bytes)
+        for q in range(4):
+            nc.vector.tensor_copy(x_plane[32 * q : 32 * q + 2, :].bitcast(I32), picked_bytes[32 * q : 32 * q + 2, :].bitcast(I32))
+        cand_bytes = sb.tile([P, C], U8, name="cand_bytes", align_bytes=64)
+        nc.vector.tensor_copy(cand_bytes[:], scale_table[:].indirect(cand_l[:]))
+        raw[0, 1] = load_w(w1, 1, shared.tile([P, 4, H // 2], F32, name="raw01", offset=0))
+        raw[1, 1] = load_w(w2, 1, shared.tile([P, 4, H // 2], F32, name="raw11", offset=4096))
+        rows4_tile = sb.tile([P, 3, 8], F32, name="rows4", tag="picked_bytes", align_bytes=64)
+        for i, (name, src) in enumerate((("sl", sl), ("th", th), ("gs", gs))):
+            rows4[name] = rows4_tile[:, i, 0:4]
+            nc.sync.dma_start(rows4[name], src.rearrange("(p t) o -> p (t o)", t=4))
+        rows4_bias = sb.tile([P, 4], F32, name="rows4_bias")
+        nc.gpsimd.tensor_tensor(rows4_bias[:], rows4["sl"], rows4["th"], ALU.mult)
+        nc.gpsimd.tensor_scalar(rows4_bias[:], rows4_bias[:], -1.0, None, ALU.mult)
+        x_codes = []
+        for name, lst in (("x_offs", offs_l), ("x_hz", hz_l)):
+            codes = sb.tile([P, S], U32, name=name, align_bytes=64)
+            nc.vector.tensor_copy(codes[:], word_table[:].indirect(lst[:]))
+            x_codes.append(codes)
+
+        cand_plane = sb.tile([P, C], U8, name="cand_plane", align_bytes=64)
+        nc.vector.tensor_copy(cand_plane[:].bitcast(I32), cand_bytes[:].bitcast(I32))
+        move_odd_rows(cand_plane, cand_bytes)
+
+        def quantise(grouped, width, name):
+            codes = sb.tile([P, width], U32, name=name + "_codes", tag=name + "_codes", align_bytes=64)
+            plane = sb.tile([P, width], U8, name=name + "_plane", align_bytes=64)
+            nc.vector.quantize_mx(out=codes[:].bitcast(FP8X4), scales=plane[:], in_=grouped)
+            return codes, plane
+
+        def copy_on(engine, dst, src):
+            if engine is nc.scalar:
+                nc.scalar.copy(dst, src)
+            else:
+                nc.vector.tensor_copy(dst, src)
+
+        def even_columns(m, half, engine):
+            name = "even_w%d%d" % (m, half)
+            grouped = sb.tile([P, P * 4], BF16, name=name, align_bytes=64)
+            copy_on(
+                engine,
+                grouped[:].rearrange("p (m e j) -> p m j e", e=2, j=4),
+                raw[m, half][:].rearrange("p j (m e two) -> p m j e two", e=2, two=2)[:, :, :, :, 0],
+            )
+            return quantise(grouped[:], P, name)
+
+        odd_grouped = [sb.tile([P, 2 * P * 4], BF16, name="odd_w%d" % m, align_bytes=64) for m in range(2)]
+
+        def odd_columns(m, half, engine):
+            copy_on(
+                engine,
+                odd_grouped[m][:].rearrange("p (e h m j) -> p h m j e", e=2, h=2, j=4)[:, half],
+                raw[m, half][:].rearrange("p j (m e two) -> p m j e two", e=2, two=2)[:, :, :, :, 1],
+            )
+
+        def project(stationary, name):
+            acc = ps.tile([P, S], F32, name=name + "_ps")
+            for m in range(2):
+                codes, plane = stationary[m]
+                nc.tensor.matmul_mx(
+                    out=acc[:], lhsT=codes.bitcast(FP8X4), lhsT_scale=plane,
+                    rhs=x_codes[m][:].bitcast(FP8X4), rhs_scale=x_plane[:, m * S : (m + 1) * S],
+                    start=(m == 0), stop=(m == 1),
+                )
+            y = sb.tile([P, S], F32, name=name)
+            nc.vector.tensor_copy(y[:], acc[:])
+            return y
+
+        def scatter_rows(y, name, tag):
+            ds = sb.tile([P, 2 * S], F32, name=name, tag=tag)
+            nc.scalar.activation(ds[:].indirect(n1_l[:]), y[:], ACT.Copy)
+            return ds
+
+        def gate(ds, lo, n, slope, bias, name):
+            sg = sb.tile([P, n], F32, name=name)
+            nc.scalar.activation(sg[:], ds[:].indirect(n2_l[:, lo // 16 : (lo + n) // 16]), ACT.Sigmoid, bias=bias, scale=slope)
+            return sg
+
+        z_even = sb.tile([P, 2, S], BF16, name="z_even")
+        z_words = [sb.tile([P, HALF * 4], BF16, name="z_words%d" % h, align_bytes=64) for h in range(2)]
+
+        def even_tile(half, engines):
+            quantised = [even_columns(m, half, engines[m]) for m in range(2)]
+            y = project([(codes[:], plane[:]) for codes, plane in quantised], "y_even%d" % half)
+            return y, scatter_rows(y, "ds_even%d" % half, "ds%d" % half)
+
+        def even_gate(half, y, ds):
+            sg = gate(ds, 0, S, even["sl"][:, half : half + 1], even_bias[:, half : half + 1], "sg_even%d" % half)
+            z = sb.tile([P, S], BF16, name="z_rows%d" % half)
+            nc.vector.scalar_tensor_tensor(z[:], y[:], even["gs"][:, half : half + 1], sg[:], ALU.mult, ALU.mult)
+            for e in range(2):
+                nc.sync.dma_start(z_even[64 * half : 64 * half + 64, e, :], z[e:P:2, :])
+
+        y_a, ds_a = even_tile(0, (nc.scalar, nc.scalar))
+        for m in range(2):
+            odd_columns(m, 0, nc.scalar)
+        even_gate(0, y_a, ds_a)
+        y_b, ds_b = even_tile(1, (nc.vector, nc.vector))
+        even_gate(1, y_b, ds_b)
+
+        odd_q = []
+        for m in range(2):
+            odd_columns(m, 1, nc.vector)
+            odd_q.append(quantise(odd_grouped[m][:], 2 * P, "odd_w%d" % m))
+        y_odd, ds_odd = [], []
+        for e in range(2):
+            cols = slice(e * P, (e + 1) * P)
+            y = project([(codes[:, cols], plane[:, cols]) for codes, plane in odd_q], "y_odd%d" % e)
+            y_odd.append(y)
+            ds_odd.append(scatter_rows(y, "ds_odd%d" % e, "ds%d" % (1 - e)))
+
+
+        cand_codes = sb.tile([P, C], U32, name="cand_codes", tag="odd_w1_codes", align_bytes=64)
+        nc.vector.tensor_copy(cand_codes[:], word_table[:].indirect(cand_l[:]))
+
+        for h in range(2):
+            nc.vector.tensor_copy(
+                z_words[h][:].rearrange("p (c i e two) -> p c e i two", i=2, e=2, two=2)[:, :, :, :, 0],
+                z_even[:, :, h * HALF : (h + 1) * HALF].rearrange("p e (c i) -> p c e i", i=2),
+            )
+
+        z_q = []
+        scores = [sb.tile([P, S], F32, name="scores%d" % c) for c in range(4)]
+        for h in range(2):
+            cols = slice(h * HALF, (h + 1) * HALF)
+            for e in range(2):
+                t = 2 * e + 1
+                sg = gate(ds_odd[e], h * HALF, HALF, rows4["sl"][:, t : t + 1], rows4_bias[:, t : t + 1], "sg_odd%d%d" % (e, h))
+                nc.vector.scalar_tensor_tensor(
+                    z_words[h][:].rearrange("p (c t) -> p c t", t=4)[:, :, t],
+                    y_odd[e][:, cols], rows4["gs"][:, t : t + 1], sg[:], ALU.mult, ALU.mult,
+                )
+            z_q.append(quantise(z_words[h][:], HALF, "z%d" % h))
+        accs = []
+        for h in range(2):
+            z_codes, z_plane = z_q[h]
+            first = ps.tile([P, HALF], F32, name="first_ps%d" % h)
+            rest = ps.tile([P, 3, HALF], F32, name="rest_ps%d" % h)
+            accs.append([first[:]] + [rest[:, c, :] for c in range(3)])
+            for c in range(4):
+                rows = slice(c * P, (c + 1) * P)
+                nc.tensor.matmul_mx(
+                    out=accs[h][c], lhsT=cand_codes[:, rows].bitcast(FP8X4), lhsT_scale=cand_plane[:, rows],
+                    rhs=z_codes[:].bitcast(FP8X4), rhs_scale=z_plane[:], start=True, stop=True,
+                )
+        for c in range(4):
+            for h in range(2):
+                nc.vector.tensor_scalar(scores[c][:, h * HALF : (h + 1) * HALF], accs[h][c], 0.0625, None, ALU.mult)
+
+        for c in range(4):
+            other = sb.tile([P, S], F32, name="other%d" % c)
+            for h in range(2):
+                nc.scalar.activation(other[:, h * HALF : (h + 1) * HALF], scores[c][:].indirect(n5_l[:, h * 8 : (h + 1) * 8]), ACT.Copy)
+            up = sb.tile([P, S], F32, name="up%d" % c)
+            dn = sb.tile([P, S], F32, name="dn%d" % c)
+            nc.vector.tensor_tensor(up[:], scores[c][:], other[:], ALU.max)
+            nc.vector.tensor_tensor(dn[:], scores[c][:], other[:], ALU.min)
+            nc.scalar.activation(pages[c][:].indirect(n3_l[:]), up[:], ACT.Copy)
+            nc.scalar.activation(pages[c][:].indirect(n4_l[:]), dn[:], ACT.Copy)
+            nc.sync.dma_start(out[c * P : (c + 1) * P, :], pages[c][:])

@@ -12,231 +12,256 @@ FP8X4 = mybir.dt.float8_e4m3fn_x4
 ALU = mybir.AluOpType
 ACT = mybir.ActivationFunctionType
 
-P = 128
 K, T, S, H, C, U = 512, 2048, 256, 512, 512, 512
-FLOPS = 2 * K * H * S * 2 + 2 * K * C * S
-HALF = S // 2
+FLOPS = 2 * 2 * K * H * S + 2 * K * C * S
+
+P = 128
+PACK = 4
+GROUP = 16
+QUAD = 32
+W_HALF = H // 2
+S_HALF = S // 2
+RAW_BYTES = PACK * W_HALF * 4
+EVEN, ODD = 0, 1
+SL, TH, GS = 0, 1, 2
 
 
 def tile_picked_thcerlpagmx_none_p_kernel(
     tc, x_words, x_scales, w1, w2, sl, th, gs, offs, hz, n1, n2, cand, n3, n4, n5, out
 ):
     nc = tc.nc
+    weights = (w1, w2)
     with ExitStack() as ctx:
         lists = ctx.enter_context(tc.tile_pool(name="lists", bufs=1))
         sb = ctx.enter_context(tc.tile_pool(name="sb", bufs=1))
         shared = ctx.enter_context(tc.tile_pool(name="shared", bufs=1))
         ps = ctx.enter_context(tc.psum_pool(name="ps", bufs=1))
 
-        def load_list(src, name):
-            tile = lists.tile(list(src.shape), U16, name=name)
-            nc.sync.dma_start(tile[:], src)
-            return tile
+        def tile(shape, dtype, name, reuses=None):
+            return sb.tile(shape, dtype, name=name, tag=reuses or name, align_bytes=64)
 
-        def load_w(w, half, raw):
-            nc.sync.dma_start(raw[:], w.rearrange("(p j) c -> p j c", j=4)[:, :, half * (H // 2) : (half + 1) * (H // 2)])
+        def load_list(src, name):
+            offsets = lists.tile(list(src.shape), U16, name=name)
+            nc.sync.dma_start(offsets[:], src)
+            return offsets
+
+        def load_weights(m, half, raw):
+            cols = slice(half * W_HALF, (half + 1) * W_HALF)
+            nc.sync.dma_start(raw[:], weights[m].rearrange("(p j) c -> p j c", j=PACK)[:, :, cols])
             return raw
 
-        scale_table = shared.tile([P, T], U8, name="scale_table", offset=3072)
+        scale_table = shared.tile([P, T], U8, name="scale_table", offset=RAW_BYTES - T // 2)
         nc.vector.memset(scale_table[:].bitcast(I32), 0)
         for e in range(2):
-            nc.scalar.dma_start(scale_table[e:P:16, :].bitcast(I32), x_scales[0][e:16:2, :].bitcast(I32))
+            nc.sync.dma_start(scale_table[e:P:GROUP, :].bitcast(I32), x_scales[0][e::2, :].bitcast(I32))
+
+        warm = tile([P, 2], F32, "warm")
+        nc.vector.memset(warm[:, 0:1], 0.0)
+        nc.scalar.activation(warm[:, 1:2], warm[:, 0:1], ACT.Sigmoid)
 
         hz_l = load_list(hz, "hz_l")
         offs_l = load_list(offs, "offs_l")
         cand_l = load_list(cand, "cand_l")
-        word_table = sb.tile([P, T], U32, name="word_table", align_bytes=64)
+        word_table = tile([P, T], U32, "word_table")
         nc.sync.dma_start(word_table[:].bitcast(I32), x_words[0].rearrange("p n t -> p (n t)").bitcast(I32))
         n1_l = load_list(n1, "n1_l")
         n2_l = load_list(n2, "n2_l")
-        raw = {}
-        raw[0, 0] = load_w(w1, 0, sb.tile([P, 4, H // 2], F32, name="raw00"))
-        raw[1, 0] = load_w(w2, 0, sb.tile([P, 4, H // 2], F32, name="raw10"))
+        raw = {(m, 0): load_weights(m, 0, tile([P, PACK, W_HALF], F32, "raw%d0" % m)) for m in range(2)}
         n5_l = load_list(n5, "n5_l")
         n3_l = load_list(n3, "n3_l")
         n4_l = load_list(n4, "n4_l")
 
-        even = {}
-        rows4 = {}
-        for name, src in (("sl", sl), ("th", th), ("gs", gs)):
-            even[name] = sb.tile([P, 2], F32, name="even_" + name)
-            with nc.allow_non_contiguous_dma(reason="one value a partition"):
-                nc.gpsimd.dma_start(even[name][:], src.rearrange("(h q two) o -> q h (two o)", h=2, two=2)[:, :, 0])
-        even_bias = sb.tile([P, 2], F32, name="even_bias")
-        nc.gpsimd.tensor_tensor(even_bias[:], even["sl"][:], even["th"][:], ALU.mult)
-        nc.gpsimd.tensor_scalar(even_bias[:], even_bias[:], -1.0, None, ALU.mult)
-
-        pages = []
-        for c in range(4):
-            page = sb.tile([P, U], F32, name="page%d" % c)
-            pages.append(page)
-
-        def move_odd_rows(plane, gathered):
+        def move_odd_runs(plane, gathered):
             for e in range(2):
-                nc.sync.dma_start(plane[2 + e : P : 32, :].bitcast(I32), gathered[16 + e : P : 32, :].bitcast(I32))
+                nc.sync.dma_start(plane[2 + e : P : QUAD, :].bitcast(I32), gathered[GROUP + e : P : QUAD, :].bitcast(I32))
 
-        picked_bytes = sb.tile([P, 2 * S], U8, name="picked_bytes", tag="picked_bytes", align_bytes=64)
+        picked_bytes = tile([P, 2 * S], U8, "picked_bytes")
         nc.vector.tensor_copy(picked_bytes[:, S:], scale_table[:].indirect(hz_l[:]))
         nc.vector.tensor_copy(picked_bytes[:, :S], scale_table[:].indirect(offs_l[:]))
-        x_plane = sb.tile([P, 2 * S], U8, name="x_plane", align_bytes=64)
+        x_plane = tile([P, 2 * S], U8, "x_plane")
         nc.vector.memset(x_plane[:].bitcast(I32), 0)
-        move_odd_rows(x_plane, picked_bytes)
-        for q in range(4):
-            nc.vector.tensor_copy(x_plane[32 * q : 32 * q + 2, :].bitcast(I32), picked_bytes[32 * q : 32 * q + 2, :].bitcast(I32))
-        cand_bytes = sb.tile([P, C], U8, name="cand_bytes", align_bytes=64)
-        nc.vector.tensor_copy(cand_bytes[:], scale_table[:].indirect(cand_l[:]))
-        raw[0, 1] = load_w(w1, 1, shared.tile([P, 4, H // 2], F32, name="raw01", offset=0))
-        raw[1, 1] = load_w(w2, 1, shared.tile([P, 4, H // 2], F32, name="raw11", offset=4096))
-        rows4_tile = sb.tile([P, 3, 8], F32, name="rows4", tag="picked_bytes", align_bytes=64)
-        for i, (name, src) in enumerate((("sl", sl), ("th", th), ("gs", gs))):
-            rows4[name] = rows4_tile[:, i, 0:4]
-            nc.sync.dma_start(rows4[name], src.rearrange("(p t) o -> p (t o)", t=4))
-        rows4_bias = sb.tile([P, 4], F32, name="rows4_bias")
-        nc.gpsimd.tensor_tensor(rows4_bias[:], rows4["sl"], rows4["th"], ALU.mult)
-        nc.gpsimd.tensor_scalar(rows4_bias[:], rows4_bias[:], -1.0, None, ALU.mult)
+        move_odd_runs(x_plane, picked_bytes)
+        for q in range(P // QUAD):
+            rows = slice(QUAD * q, QUAD * q + 2)
+            nc.vector.tensor_copy(x_plane[rows, :].bitcast(I32), picked_bytes[rows, :].bitcast(I32))
+        cand_table = tile([P, T], U8, "cand_table")
+        nc.vector.tensor_copy(cand_table[:].bitcast(I32), scale_table[:].bitcast(I32))
+        for m in range(2):
+            second = shared.tile([P, PACK, W_HALF], F32, name="raw%d1" % m, offset=m * RAW_BYTES)
+            raw[m, 1] = load_weights(m, 1, second)
+
+        later = tile([P, 4, 8], F32, "later_rows", reuses="picked_bytes")
+        per_row = {
+            (EVEN, SL): tile([P, 2], F32, "even_sl")[:],
+            (EVEN, TH): tile([P, 2], F32, "even_th")[:],
+            (EVEN, GS): later[:, 0, 0:2],
+            (ODD, GS): later[:, 1, 0:2],
+            (ODD, SL): later[:, 2, 0:2],
+            (ODD, TH): later[:, 3, 0:2],
+        }
+        row_order = {EVEN: "(i p two) o -> p i (two o)", ODD: "(p i two) o -> p i (two o)"}
+        with nc.allow_non_contiguous_dma(reason="one value for each partition and tile"):
+            for (kind, which), dst in per_row.items():
+                queue = nc.gpsimd if kind == EVEN and which != GS else nc.sync
+                queue.dma_start(dst, (sl, th, gs)[which].rearrange(row_order[kind], i=2, two=2)[:, :, kind])
+        bias = []
+        for kind in (EVEN, ODD):
+            minus_sl_th = tile([P, 2], F32, "bias%d" % kind)
+            nc.gpsimd.tensor_tensor(minus_sl_th[:], per_row[kind, SL], per_row[kind, TH], ALU.mult)
+            nc.gpsimd.tensor_scalar(minus_sl_th[:], minus_sl_th[:], -1.0, None, ALU.mult)
+            bias.append(minus_sl_th)
+
         x_codes = []
-        for name, lst in (("x_offs", offs_l), ("x_hz", hz_l)):
-            codes = sb.tile([P, S], U32, name=name, align_bytes=64)
-            nc.vector.tensor_copy(codes[:], word_table[:].indirect(lst[:]))
+        for name, offsets in (("x_offs", offs_l), ("x_hz", hz_l)):
+            codes = tile([P, S], U32, name)
+            nc.vector.tensor_copy(codes[:], word_table[:].indirect(offsets[:]))
             x_codes.append(codes)
+        cand_bytes = tile([P, C], U8, "cand_bytes")
+        nc.vector.tensor_copy(cand_bytes[:], cand_table[:].indirect(cand_l[:]))
 
-        cand_plane = sb.tile([P, C], U8, name="cand_plane", align_bytes=64)
-        nc.vector.tensor_copy(cand_plane[:].bitcast(I32), cand_bytes[:].bitcast(I32))
-        move_odd_rows(cand_plane, cand_bytes)
-
-        def quantise(grouped, width, name):
-            codes = sb.tile([P, width], U32, name=name + "_codes", tag=name + "_codes", align_bytes=64)
-            plane = sb.tile([P, width], U8, name=name + "_plane", align_bytes=64)
-            nc.vector.quantize_mx(out=codes[:].bitcast(FP8X4), scales=plane[:], in_=grouped)
+        def quantise(grouped, name):
+            width = grouped.shape[1] // PACK
+            codes = tile([P, width], U32, name + "_codes")
+            plane = tile([P, width], U8, name + "_plane")
+            nc.vector.quantize_mx(out=codes[:].bitcast(FP8X4), scales=plane[:], in_=grouped[:])
             return codes, plane
 
-        def copy_on(engine, dst, src):
-            if engine is nc.scalar:
-                nc.scalar.copy(dst, src)
-            else:
-                nc.vector.tensor_copy(dst, src)
+        def weight_columns(m, half, kind):
+            return raw[m, half][:].rearrange("p j (a e two) -> p a j e two", e=2, two=2)[:, :, :, :, kind]
 
-        def even_columns(m, half, engine):
+        def even_weights(m, half, copy):
             name = "even_w%d%d" % (m, half)
-            grouped = sb.tile([P, P * 4], BF16, name=name, align_bytes=64)
-            copy_on(
-                engine,
-                grouped[:].rearrange("p (m e j) -> p m j e", e=2, j=4),
-                raw[m, half][:].rearrange("p j (m e two) -> p m j e two", e=2, two=2)[:, :, :, :, 0],
-            )
-            return quantise(grouped[:], P, name)
+            grouped = tile([P, P * PACK], BF16, name)
+            copy(grouped[:].rearrange("p (a e j) -> p a j e", e=2, j=PACK), weight_columns(m, half, EVEN))
+            return quantise(grouped, name)
 
-        odd_grouped = [sb.tile([P, 2 * P * 4], BF16, name="odd_w%d" % m, align_bytes=64) for m in range(2)]
+        def odd_weights(m, half, copy):
+            dst = odd_grouped[m][:].rearrange("p (e h a j) -> p h a j e", e=2, h=2, j=PACK)[:, half]
+            copy(dst, weight_columns(m, half, ODD))
 
-        def odd_columns(m, half, engine):
-            copy_on(
-                engine,
-                odd_grouped[m][:].rearrange("p (e h m j) -> p h m j e", e=2, h=2, j=4)[:, half],
-                raw[m, half][:].rearrange("p j (m e two) -> p m j e two", e=2, two=2)[:, :, :, :, 1],
-            )
-
-        def project(stationary, name):
+        def project(quantised, cols, name, copy):
             acc = ps.tile([P, S], F32, name=name + "_ps")
-            for m in range(2):
-                codes, plane = stationary[m]
+            for m, (codes, plane) in enumerate(quantised):
                 nc.tensor.matmul_mx(
-                    out=acc[:], lhsT=codes.bitcast(FP8X4), lhsT_scale=plane,
-                    rhs=x_codes[m][:].bitcast(FP8X4), rhs_scale=x_plane[:, m * S : (m + 1) * S],
-                    start=(m == 0), stop=(m == 1),
+                    out=acc[:],
+                    lhsT=codes[:, cols].bitcast(FP8X4),
+                    lhsT_scale=plane[:, cols],
+                    rhs=x_codes[m][:].bitcast(FP8X4),
+                    rhs_scale=x_plane[:, m * S : (m + 1) * S],
+                    start=(m == 0),
+                    stop=(m == 1),
                 )
-            y = sb.tile([P, S], F32, name=name)
-            nc.vector.tensor_copy(y[:], acc[:])
-            return y
+            y = tile([P, S], F32, name)
+            copy(y[:], acc[:])
+            return acc, y
 
-        def scatter_rows(y, name, tag):
-            ds = sb.tile([P, 2 * S], F32, name=name, tag=tag)
+        def send(y, name, reuses=None):
+            ds = tile([P, 2 * S], F32, name, reuses)
             nc.scalar.activation(ds[:].indirect(n1_l[:]), y[:], ACT.Copy)
             return ds
 
-        def gate(ds, lo, n, slope, bias, name):
-            sg = sb.tile([P, n], F32, name=name)
-            nc.scalar.activation(sg[:], ds[:].indirect(n2_l[:, lo // 16 : (lo + n) // 16]), ACT.Sigmoid, bias=bias, scale=slope)
-            return sg
-
-        z_even = sb.tile([P, 2, S], BF16, name="z_even")
-        z_words = [sb.tile([P, HALF * 4], BF16, name="z_words%d" % h, align_bytes=64) for h in range(2)]
-
-        def even_tile(half, engines):
-            quantised = [even_columns(m, half, engines[m]) for m in range(2)]
-            y = project([(codes[:], plane[:]) for codes, plane in quantised], "y_even%d" % half)
-            return y, scatter_rows(y, "ds_even%d" % half, "ds%d" % half)
-
-        def even_gate(half, y, ds):
-            sg = gate(ds, 0, S, even["sl"][:, half : half + 1], even_bias[:, half : half + 1], "sg_even%d" % half)
-            z = sb.tile([P, S], BF16, name="z_rows%d" % half)
-            nc.vector.scalar_tensor_tensor(z[:], y[:], even["gs"][:, half : half + 1], sg[:], ALU.mult, ALU.mult)
-            for e in range(2):
-                nc.sync.dma_start(z_even[64 * half : 64 * half + 64, e, :], z[e:P:2, :])
-
-        y_a, ds_a = even_tile(0, (nc.scalar, nc.scalar))
-        for m in range(2):
-            odd_columns(m, 0, nc.scalar)
-        even_gate(0, y_a, ds_a)
-        y_b, ds_b = even_tile(1, (nc.vector, nc.vector))
-        even_gate(1, y_b, ds_b)
-
-        odd_q = []
-        for m in range(2):
-            odd_columns(m, 1, nc.vector)
-            odd_q.append(quantise(odd_grouped[m][:], 2 * P, "odd_w%d" % m))
-        y_odd, ds_odd = [], []
-        for e in range(2):
-            cols = slice(e * P, (e + 1) * P)
-            y = project([(codes[:, cols], plane[:, cols]) for codes, plane in odd_q], "y_odd%d" % e)
-            y_odd.append(y)
-            ds_odd.append(scatter_rows(y, "ds_odd%d" % e, "ds%d" % (1 - e)))
-
-
-        cand_codes = sb.tile([P, C], U32, name="cand_codes", tag="odd_w1_codes", align_bytes=64)
-        nc.vector.tensor_copy(cand_codes[:], word_table[:].indirect(cand_l[:]))
-
-        for h in range(2):
-            nc.vector.tensor_copy(
-                z_words[h][:].rearrange("p (c i e two) -> p c e i two", i=2, e=2, two=2)[:, :, :, :, 0],
-                z_even[:, :, h * HALF : (h + 1) * HALF].rearrange("p e (c i) -> p c e i", i=2),
+        def gate(sg, ds, kind, i, lo):
+            nc.scalar.activation(
+                sg,
+                ds[:].indirect(n2_l[:, lo // GROUP : (lo + sg.shape[1]) // GROUP]),
+                ACT.Sigmoid,
+                bias=bias[kind][:, i : i + 1],
+                scale=per_row[kind, SL][:, i : i + 1],
             )
 
-        z_q = []
-        scores = [sb.tile([P, S], F32, name="scores%d" % c) for c in range(4)]
+        left = tile([P, PACK, S], F32, "left")
+        right = [tile([P, PACK, S_HALF], F32, "right%d" % h) for h in range(2)]
         for h in range(2):
-            cols = slice(h * HALF, (h + 1) * HALF)
-            for e in range(2):
-                t = 2 * e + 1
-                sg = gate(ds_odd[e], h * HALF, HALF, rows4["sl"][:, t : t + 1], rows4_bias[:, t : t + 1], "sg_odd%d%d" % (e, h))
-                nc.vector.scalar_tensor_tensor(
-                    z_words[h][:].rearrange("p (c t) -> p c t", t=4)[:, :, t],
-                    y_odd[e][:, cols], rows4["gs"][:, t : t + 1], sg[:], ALU.mult, ALU.mult,
-                )
-            z_q.append(quantise(z_words[h][:], HALF, "z%d" % h))
-        accs = []
-        for h in range(2):
-            z_codes, z_plane = z_q[h]
-            first = ps.tile([P, HALF], F32, name="first_ps%d" % h)
-            rest = ps.tile([P, 3, HALF], F32, name="rest_ps%d" % h)
-            accs.append([first[:]] + [rest[:, c, :] for c in range(3)])
-            for c in range(4):
-                rows = slice(c * P, (c + 1) * P)
-                nc.tensor.matmul_mx(
-                    out=accs[h][c], lhsT=cand_codes[:, rows].bitcast(FP8X4), lhsT_scale=cand_plane[:, rows],
-                    rhs=z_codes[:].bitcast(FP8X4), rhs_scale=z_plane[:], start=True, stop=True,
-                )
-        for c in range(4):
-            for h in range(2):
-                nc.vector.tensor_scalar(scores[c][:, h * HALF : (h + 1) * HALF], accs[h][c], 0.0625, None, ALU.mult)
+            nc.vector.memset(right[h][:, EVEN::2, :], 1.0)
 
-        for c in range(4):
-            other = sb.tile([P, S], F32, name="other%d" % c)
+        def even_z(half, y, sg, reuses):
+            z = tile([P, S], F32, "z_rows%d" % half, reuses)
+            nc.vector.scalar_tensor_tensor(z[:], y[:], per_row[EVEN, GS][:, half : half + 1], sg[:], ALU.mult, ALU.mult)
+            for e in range(2):
+                nc.sync.dma_start(left[half * P // 2 : (half + 1) * P // 2, 2 * e, :], z[e:P:2, :])
+
+        everything = slice(0, P)
+        y_a = project([even_weights(m, 0, nc.scalar.copy) for m in range(2)], everything, "y_even0", nc.scalar.copy)[1]
+        ds_a = send(y_a, "ds_even0")
+        odd_grouped = [
+            tile([P, 2 * P * PACK], BF16, "odd_w0"),
+            tile([P, 2 * P * PACK], BF16, "odd_w1", reuses="even_w10_codes"),
+        ]
+        for m in range(2):
+            odd_weights(m, 0, nc.scalar.copy)
+        cand_plane = tile([P, C], U8, "cand_plane", reuses="even_w00_codes")
+        nc.vector.tensor_copy(cand_plane[:].bitcast(I32), cand_bytes[:].bitcast(I32))
+        move_odd_runs(cand_plane, cand_bytes)
+
+        even_q = [even_weights(0, 1, nc.vector.tensor_copy)]
+        odd_weights(0, 1, nc.vector.tensor_copy)
+        odd_q = [quantise(odd_grouped[0], "odd_w0")]
+        even_q.append(even_weights(1, 1, nc.vector.tensor_copy))
+        y_b = project(even_q, everything, "y_even1", nc.vector.tensor_copy)[1]
+        ds_b = send(y_b, "ds_even1")
+        cand_codes = tile([P, C], U32, "cand_codes", reuses="even_w11_codes")
+        nc.vector.tensor_copy(cand_codes[:], word_table[:].indirect(cand_l[:]))
+        sg_a = tile([P, S], F32, "sg_even0", reuses="word_table")
+        gate(sg_a[:], ds_a, EVEN, 0, 0)
+        sg_b = tile([P, S], F32, "sg_even1")
+        gate(sg_b[:], ds_b, EVEN, 1, 0)
+        odd_weights(1, 1, nc.vector.tensor_copy)
+        odd_q.append(quantise(odd_grouped[1], "odd_w1"))
+
+        sums_odd, ds_odd = [], []
+        for i in range(2):
+            acc, y = project(odd_q, slice(i * P, (i + 1) * P), "y_odd%d" % i, nc.vector.tensor_copy)
+            sums_odd.append(acc)
+            ds_odd.append(send(y, "ds_odd%d" % i, reuses="ds_even%d" % i))
+        for i in range(2):
+            nc.vector.tensor_scalar(left[:, 2 * i + 1, :], sums_odd[i][:], per_row[ODD, GS][:, i : i + 1], None, ALU.mult)
+        even_z(0, y_a, sg_a, reuses="x_hz")
+        even_z(1, y_b, sg_b, reuses="odd_w1_codes")
+
+        z_q = []
+        for h in range(2):
+            for i in range(2):
+                gate(right[h][:, 2 * i + 1, :], ds_odd[i], ODD, i, h * S_HALF)
+            z_grouped = tile([P, S_HALF * PACK], BF16, "z_grouped%d" % h)
+            nc.vector.tensor_tensor(
+                z_grouped[:].rearrange("p (c n t) -> p c t n", n=4, t=PACK),
+                left[:, :, h * S_HALF : (h + 1) * S_HALF].rearrange("p t (c n) -> p c t n", n=4),
+                right[h][:].rearrange("p t (c n) -> p c t n", n=4),
+                ALU.mult,
+            )
+            z_q.append(quantise(z_grouped, "z%d" % h))
+
+        sums = []
+        for h, (z_codes, z_plane) in enumerate(z_q):
+            first = ps.tile([P, S_HALF], F32, name="first_ps%d" % h)
+            rest = ps.tile([P, C // P - 1, S_HALF], F32, name="rest_ps%d" % h)
+            sums.append([first[:]] + [rest[:, c, :] for c in range(C // P - 1)])
+            for c in range(C // P):
+                picked = slice(c * P, (c + 1) * P)
+                nc.tensor.matmul_mx(
+                    out=sums[h][c],
+                    lhsT=cand_codes[:, picked].bitcast(FP8X4),
+                    lhsT_scale=cand_plane[:, picked],
+                    rhs=z_codes[:].bitcast(FP8X4),
+                    rhs_scale=z_plane[:],
+                    start=True,
+                    stop=True,
+                )
+        scores = [tile([P, S], F32, "scores%d" % c) for c in range(C // P)]
+        for c in range(C // P):
             for h in range(2):
-                nc.scalar.activation(other[:, h * HALF : (h + 1) * HALF], scores[c][:].indirect(n5_l[:, h * 8 : (h + 1) * 8]), ACT.Copy)
-            up = sb.tile([P, S], F32, name="up%d" % c)
-            dn = sb.tile([P, S], F32, name="dn%d" % c)
+                nc.vector.tensor_scalar(scores[c][:, h * S_HALF : (h + 1) * S_HALF], sums[h][c], 0.0625, None, ALU.mult)
+
+        for c in range(C // P):
+            other = tile([P, S], F32, "other%d" % c)
+            for h in range(2):
+                entries = n5_l[:, h * S_HALF // GROUP : (h + 1) * S_HALF // GROUP]
+                nc.scalar.activation(other[:, h * S_HALF : (h + 1) * S_HALF], scores[c][:].indirect(entries), ACT.Copy)
+            up = tile([P, S], F32, "up%d" % c)
+            dn = tile([P, S], F32, "dn%d" % c)
             nc.vector.tensor_tensor(up[:], scores[c][:], other[:], ALU.max)
             nc.vector.tensor_tensor(dn[:], scores[c][:], other[:], ALU.min)
-            nc.scalar.activation(pages[c][:].indirect(n3_l[:]), up[:], ACT.Copy)
-            nc.scalar.activation(pages[c][:].indirect(n4_l[:]), dn[:], ACT.Copy)
-            nc.sync.dma_start(out[c * P : (c + 1) * P, :], pages[c][:])
+            page = tile([P, U], F32, "page%d" % c)
+            nc.scalar.activation(page[:].indirect(n3_l[:]), up[:], ACT.Copy)
+            nc.scalar.activation(page[:].indirect(n4_l[:]), dn[:], ACT.Copy)
+            nc.sync.dma_start(out[c * P : (c + 1) * P, :], page[:])

@@ -90,20 +90,12 @@ def tile_picked_thcerlpagmx_none_p_kernel(
             second = shared.tile([P, PACK, W_HALF], F32, name="raw%d1" % m, offset=m * RAW_BYTES)
             raw[m, 1] = load_weights(m, 1, second)
 
-        later = tile([P, 4, 8], F32, "later_rows", reuses="picked_bytes")
-        per_row = {
-            (EVEN, SL): tile([P, 2], F32, "even_sl")[:],
-            (EVEN, TH): tile([P, 2], F32, "even_th")[:],
-            (EVEN, GS): later[:, 0, 0:2],
-            (ODD, GS): later[:, 1, 0:2],
-            (ODD, SL): later[:, 2, 0:2],
-            (ODD, TH): later[:, 3, 0:2],
-        }
+        row_values = tile([P, 2, 3, 8], F32, "row_values", reuses="picked_bytes")
+        per_row = {(kind, which): row_values[:, kind, which, 0:2] for kind in (EVEN, ODD) for which in (SL, TH, GS)}
         row_order = {EVEN: "(i p two) o -> p i (two o)", ODD: "(p i two) o -> p i (two o)"}
         with nc.allow_non_contiguous_dma(reason="one value for each partition and tile"):
             for (kind, which), dst in per_row.items():
-                queue = nc.gpsimd if kind == EVEN and which != GS else nc.sync
-                queue.dma_start(dst, (sl, th, gs)[which].rearrange(row_order[kind], i=2, two=2)[:, :, kind])
+                nc.sync.dma_start(dst, (sl, th, gs)[which].rearrange(row_order[kind], i=2, two=2)[:, :, kind])
         bias = []
         for kind in (EVEN, ODD):
             minus_sl_th = tile([P, 2], F32, "bias%d" % kind)
@@ -129,10 +121,14 @@ def tile_picked_thcerlpagmx_none_p_kernel(
         def weight_columns(m, half, kind):
             return raw[m, half][:].rearrange("p j (a e two) -> p a j e two", e=2, two=2)[:, :, :, :, kind]
 
-        def even_weights(m, half, copy):
+        def even_weights(m, half, copies, reuses=None):
             name = "even_w%d%d" % (m, half)
-            grouped = tile([P, P * PACK], BF16, name)
-            copy(grouped[:].rearrange("p (a e j) -> p a j e", e=2, j=PACK), weight_columns(m, half, EVEN))
+            grouped = tile([P, P * PACK], BF16, name, reuses)
+            dst = grouped[:].rearrange("p (a e j) -> p a j e", e=2, j=PACK)
+            share = P // 2 // len(copies)
+            for n, copy in enumerate(copies):
+                part = slice(n * share, (n + 1) * share)
+                copy(dst[:, part], weight_columns(m, half, EVEN)[:, part])
             return quantise(grouped, name)
 
         def odd_weights(m, half, copy):
@@ -181,7 +177,11 @@ def tile_picked_thcerlpagmx_none_p_kernel(
                 nc.sync.dma_start(left[half * P // 2 : (half + 1) * P // 2, 2 * e, :], z[e:P:2, :])
 
         everything = slice(0, P)
-        y_a = project([even_weights(m, 0, nc.scalar.copy) for m in range(2)], everything, "y_even0", nc.scalar.copy)[1]
+        first_q = [
+            even_weights(0, 0, [nc.scalar.copy]),
+            even_weights(1, 0, [nc.scalar.copy, nc.vector.tensor_copy], reuses="cand_table"),
+        ]
+        y_a = project(first_q, everything, "y_even0", nc.scalar.copy)[1]
         ds_a = send(y_a, "ds_even0")
         odd_grouped = [
             tile([P, 2 * P * PACK], BF16, "odd_w0"),
@@ -193,10 +193,10 @@ def tile_picked_thcerlpagmx_none_p_kernel(
         nc.vector.tensor_copy(cand_plane[:].bitcast(I32), cand_bytes[:].bitcast(I32))
         move_odd_runs(cand_plane, cand_bytes)
 
-        even_q = [even_weights(0, 1, nc.vector.tensor_copy)]
+        even_q = [even_weights(0, 1, [nc.vector.tensor_copy])]
         odd_weights(0, 1, nc.vector.tensor_copy)
         odd_q = [quantise(odd_grouped[0], "odd_w0")]
-        even_q.append(even_weights(1, 1, nc.vector.tensor_copy))
+        even_q.append(even_weights(1, 1, [nc.vector.tensor_copy]))
         y_b = project(even_q, everything, "y_even1", nc.vector.tensor_copy)[1]
         ds_b = send(y_b, "ds_even1")
         cand_codes = tile([P, C], U32, "cand_codes", reuses="even_w11_codes")

from contextlib import ExitStack

import concourse.mybir as mybir

F32 = mybir.dt.float32
BF16 = mybir.dt.bfloat16
I32 = mybir.dt.int32
U32 = mybir.dt.uint32
U16 = mybir.dt.uint16
U8 = mybir.dt.uint8
FP8X4 = mybir.dt.float8_e4m3fn_x4
ALU = mybir.AluOpType
ACT = mybir.ActivationFunctionType

K, T, S, H, C, U = 512, 2048, 256, 512, 512, 512
FLOPS = 2 * 2 * K * H * S + 2 * K * C * S

P = 128
PACK = 4
GROUP = 16
QUAD = 32
W_HALF = H // 2
S_HALF = S // 2
RAW_BYTES = PACK * W_HALF * 4
EVEN, ODD = 0, 1
SL, TH, GS = 0, 1, 2


def tile_picked_thcerlpagmx_none_p_kernel(
    tc, x_words, x_scales, w1, w2, sl, th, gs, offs, hz, n1, n2, cand, n3, n4, n5, out
):
    nc = tc.nc
    weights = (w1, w2)
    with ExitStack() as ctx:
        lists = ctx.enter_context(tc.tile_pool(name="lists", bufs=1))
        sb = ctx.enter_context(tc.tile_pool(name="sb", bufs=1))
        shared = ctx.enter_context(tc.tile_pool(name="shared", bufs=1))
        ps = ctx.enter_context(tc.psum_pool(name="ps", bufs=1))

        def tile(shape, dtype, name, reuses=None):
            return sb.tile(shape, dtype, name=name, tag=reuses or name, align_bytes=64)

        def load_list(src, name):
            offsets = lists.tile(list(src.shape), U16, name=name)
            nc.sync.dma_start(offsets[:], src)
            return offsets

        def load_weights(m, half, raw):
            cols = slice(half * W_HALF, (half + 1) * W_HALF)
            nc.sync.dma_start(raw[:], weights[m].rearrange("(p j) c -> p j c", j=PACK)[:, :, cols])
            return raw

        scale_table = shared.tile([P, T], U8, name="scale_table", offset=RAW_BYTES - T // 2)
        nc.vector.memset(scale_table[:].bitcast(I32), 0)
        for e in range(2):
            nc.sync.dma_start(scale_table[e:P:GROUP, :].bitcast(I32), x_scales[0][e::2, :].bitcast(I32))

        warm = tile([P, 2], F32, "warm")
        nc.vector.memset(warm[:, 0:1], 0.0)
        nc.scalar.activation(warm[:, 1:2], warm[:, 0:1], ACT.Sigmoid)

        hz_l = load_list(hz, "hz_l")
        offs_l = load_list(offs, "offs_l")
        cand_l = load_list(cand, "cand_l")
        word_table = tile([P, T], U32, "word_table")
        nc.sync.dma_start(word_table[:].bitcast(I32), x_words[0].rearrange("p n t -> p (n t)").bitcast(I32))
        n1_l = load_list(n1, "n1_l")
        n2_l = load_list(n2, "n2_l")
        raw = {(m, 0): load_weights(m, 0, tile([P, PACK, W_HALF], F32, "raw%d0" % m)) for m in range(2)}
        n5_l = load_list(n5, "n5_l")
        n3_l = load_list(n3, "n3_l")
        n4_l = load_list(n4, "n4_l")

        def move_odd_runs(plane, gathered):
            for e in range(2):
                nc.sync.dma_start(plane[2 + e : P : QUAD, :].bitcast(I32), gathered[GROUP + e : P : QUAD, :].bitcast(I32))

        picked_bytes = tile([P, 2 * S], U8, "picked_bytes")
        nc.vector.tensor_copy(picked_bytes[:, S:], scale_table[:].indirect(hz_l[:]))
        nc.vector.tensor_copy(picked_bytes[:, :S], scale_table[:].indirect(offs_l[:]))
        x_plane = tile([P, 2 * S], U8, "x_plane")
        nc.vector.memset(x_plane[:].bitcast(I32), 0)
        move_odd_runs(x_plane, picked_bytes)
        for q in range(P // QUAD):
            rows = slice(QUAD * q, QUAD * q + 2)
            nc.vector.tensor_copy(x_plane[rows, :].bitcast(I32), picked_bytes[rows, :].bitcast(I32))
        cand_table = tile([P, T], U8, "cand_table")
        nc.vector.tensor_copy(cand_table[:].bitcast(I32), scale_table[:].bitcast(I32))
        for m in range(2):
            second = shared.tile([P, PACK, W_HALF], F32, name="raw%d1" % m, offset=m * RAW_BYTES)
            raw[m, 1] = load_weights(m, 1, second)

        row_values = tile([P, 2, 3, 8], F32, "row_values", reuses="picked_bytes")
        per_row = {(kind, which): row_values[:, kind, which, 0:2] for kind in (EVEN, ODD) for which in (SL, TH, GS)}
        row_order = {EVEN: "(i p two) o -> p i (two o)", ODD: "(p i two) o -> p i (two o)"}
        with nc.allow_non_contiguous_dma(reason="one value for each partition and tile"):
            for (kind, which), dst in per_row.items():
                nc.sync.dma_start(dst, (sl, th, gs)[which].rearrange(row_order[kind], i=2, two=2)[:, :, kind])
        bias = []
        for kind in (EVEN, ODD):
            minus_sl_th = tile([P, 2], F32, "bias%d" % kind)
            nc.gpsimd.tensor_tensor(minus_sl_th[:], per_row[kind, SL], per_row[kind, TH], ALU.mult)
            nc.gpsimd.tensor_scalar(minus_sl_th[:], minus_sl_th[:], -1.0, None, ALU.mult)
            bias.append(minus_sl_th)

        x_codes = []
        for name, offsets in (("x_offs", offs_l), ("x_hz", hz_l)):
            codes = tile([P, S], U32, name)
            nc.vector.tensor_copy(codes[:], word_table[:].indirect(offsets[:]))
            x_codes.append(codes)
        cand_bytes = tile([P, C], U8, "cand_bytes")
        nc.vector.tensor_copy(cand_bytes[:], cand_table[:].indirect(cand_l[:]))

        def quantise(grouped, name):
            width = grouped.shape[1] // PACK
            codes = tile([P, width], U32, name + "_codes")
            plane = tile([P, width], U8, name + "_plane")
            nc.vector.quantize_mx(out=codes[:].bitcast(FP8X4), scales=plane[:], in_=grouped[:])
            return codes, plane

        def weight_columns(m, half, kind):
            return raw[m, half][:].rearrange("p j (a e two) -> p a j e two", e=2, two=2)[:, :, :, :, kind]

        def even_weights(m, half, copies, reuses=None):
            name = "even_w%d%d" % (m, half)
            grouped = tile([P, P * PACK], BF16, name, reuses)
            dst = grouped[:].rearrange("p (a e j) -> p a j e", e=2, j=PACK)
            share = P // 2 // len(copies)
            for n, copy in enumerate(copies):
                part = slice(n * share, (n + 1) * share)
                copy(dst[:, part], weight_columns(m, half, EVEN)[:, part])
            return quantise(grouped, name)

        def odd_weights(m, half, copy):
            dst = odd_grouped[m][:].rearrange("p (e h a j) -> p h a j e", e=2, h=2, j=PACK)[:, half]
            copy(dst, weight_columns(m, half, ODD))

        def project(quantised, cols, name, copy):
            acc = ps.tile([P, S], F32, name=name + "_ps")
            for m, (codes, plane) in enumerate(quantised):
                nc.tensor.matmul_mx(
                    out=acc[:],
                    lhsT=codes[:, cols].bitcast(FP8X4),
                    lhsT_scale=plane[:, cols],
                    rhs=x_codes[m][:].bitcast(FP8X4),
                    rhs_scale=x_plane[:, m * S : (m + 1) * S],
                    start=(m == 0),
                    stop=(m == 1),
                )
            y = tile([P, S], F32, name)
            copy(y[:], acc[:])
            return acc, y

        def send(y, name, reuses=None):
            ds = tile([P, 2 * S], F32, name, reuses)
            nc.scalar.activation(ds[:].indirect(n1_l[:]), y[:], ACT.Copy)
            return ds

        def gate(sg, ds, kind, i, lo):
            nc.scalar.activation(
                sg,
                ds[:].indirect(n2_l[:, lo // GROUP : (lo + sg.shape[1]) // GROUP]),
                ACT.Sigmoid,
                bias=bias[kind][:, i : i + 1],
                scale=per_row[kind, SL][:, i : i + 1],
            )

        left = tile([P, PACK, S], F32, "left")
        right = [tile([P, PACK, S_HALF], F32, "right%d" % h) for h in range(2)]
        for h in range(2):
            nc.vector.memset(right[h][:, EVEN::2, :], 1.0)

        def even_z(half, y, sg, reuses):
            z = tile([P, S], F32, "z_rows%d" % half, reuses)
            nc.vector.scalar_tensor_tensor(z[:], y[:], per_row[EVEN, GS][:, half : half + 1], sg[:], ALU.mult, ALU.mult)
            for e in range(2):
                nc.sync.dma_start(left[half * P // 2 : (half + 1) * P // 2, 2 * e, :], z[e:P:2, :])

        everything = slice(0, P)
        first_q = [
            even_weights(0, 0, [nc.scalar.copy]),
            even_weights(1, 0, [nc.scalar.copy, nc.vector.tensor_copy], reuses="cand_table"),
        ]
        y_a = project(first_q, everything, "y_even0", nc.scalar.copy)[1]
        ds_a = send(y_a, "ds_even0")
        odd_grouped = [
            tile([P, 2 * P * PACK], BF16, "odd_w0"),
            tile([P, 2 * P * PACK], BF16, "odd_w1", reuses="even_w10_codes"),
        ]
        for m in range(2):
            odd_weights(m, 0, nc.scalar.copy)
        cand_plane = tile([P, C], U8, "cand_plane", reuses="even_w00_codes")
        nc.vector.tensor_copy(cand_plane[:].bitcast(I32), cand_bytes[:].bitcast(I32))
        move_odd_runs(cand_plane, cand_bytes)

        even_q = [even_weights(0, 1, [nc.vector.tensor_copy])]
        odd_weights(0, 1, nc.vector.tensor_copy)
        odd_q = [quantise(odd_grouped[0], "odd_w0")]
        even_q.append(even_weights(1, 1, [nc.vector.tensor_copy]))
        y_b = project(even_q, everything, "y_even1", nc.vector.tensor_copy)[1]
        ds_b = send(y_b, "ds_even1")
        cand_codes = tile([P, C], U32, "cand_codes", reuses="even_w11_codes")
        nc.vector.tensor_copy(cand_codes[:], word_table[:].indirect(cand_l[:]))
        sg_a = tile([P, S], F32, "sg_even0", reuses="word_table")
        gate(sg_a[:], ds_a, EVEN, 0, 0)
        sg_b = tile([P, S], F32, "sg_even1")
        gate(sg_b[:], ds_b, EVEN, 1, 0)
        odd_weights(1, 1, nc.vector.tensor_copy)
        odd_q.append(quantise(odd_grouped[1], "odd_w1"))

        sums_odd, ds_odd = [], []
        for i in range(2):
            acc, y = project(odd_q, slice(i * P, (i + 1) * P), "y_odd%d" % i, nc.vector.tensor_copy)
            sums_odd.append(acc)
            ds_odd.append(send(y, "ds_odd%d" % i, reuses="ds_even%d" % i))
        for i in range(2):
            nc.vector.tensor_scalar(left[:, 2 * i + 1, :], sums_odd[i][:], per_row[ODD, GS][:, i : i + 1], None, ALU.mult)
        even_z(0, y_a, sg_a, reuses="x_hz")
        even_z(1, y_b, sg_b, reuses="odd_w1_codes")

        z_q = []
        for h in range(2):
            for i in range(2):
                gate(right[h][:, 2 * i + 1, :], ds_odd[i], ODD, i, h * S_HALF)
            z_grouped = tile([P, S_HALF * PACK], BF16, "z_grouped%d" % h)
            nc.vector.tensor_tensor(
                z_grouped[:].rearrange("p (c n t) -> p c t n", n=4, t=PACK),
                left[:, :, h * S_HALF : (h + 1) * S_HALF].rearrange("p t (c n) -> p c t n", n=4),
                right[h][:].rearrange("p t (c n) -> p c t n", n=4),
                ALU.mult,
            )
            z_q.append(quantise(z_grouped, "z%d" % h))

        sums = []
        for h, (z_codes, z_plane) in enumerate(z_q):
            first = ps.tile([P, S_HALF], F32, name="first_ps%d" % h)
            rest = ps.tile([P, C // P - 1, S_HALF], F32, name="rest_ps%d" % h)
            sums.append([first[:]] + [rest[:, c, :] for c in range(C // P - 1)])
            for c in range(C // P):
                picked = slice(c * P, (c + 1) * P)
                nc.tensor.matmul_mx(
                    out=sums[h][c],
                    lhsT=cand_codes[:, picked].bitcast(FP8X4),
                    lhsT_scale=cand_plane[:, picked],
                    rhs=z_codes[:].bitcast(FP8X4),
                    rhs_scale=z_plane[:],
                    start=True,
                    stop=True,
                )
        scores = [tile([P, S], F32, "scores%d" % c) for c in range(C // P)]
        for c in range(C // P):
            for h in range(2):
                nc.vector.tensor_scalar(scores[c][:, h * S_HALF : (h + 1) * S_HALF], sums[h][c], 0.0625, None, ALU.mult)

        for c in range(C // P):
            other = tile([P, S], F32, "other%d" % c)
            for h in range(2):
                entries = n5_l[:, h * S_HALF // GROUP : (h + 1) * S_HALF // GROUP]
                nc.scalar.activation(other[:, h * S_HALF : (h + 1) * S_HALF], scores[c][:].indirect(entries), ACT.Copy)
            up = tile([P, S], F32, "up%d" % c)
            dn = tile([P, S], F32, "dn%d" % c)
            nc.vector.tensor_tensor(up[:], scores[c][:], other[:], ALU.max)
            nc.vector.tensor_tensor(dn[:], scores[c][:], other[:], ALU.min)
            page = tile([P, U], F32, "page%d" % c)
            nc.scalar.activation(page[:].indirect(n3_l[:]), up[:], ACT.Copy)
            nc.scalar.activation(page[:].indirect(n4_l[:]), dn[:], ACT.Copy)
            nc.sync.dma_start(out[c * P : (c + 1) * P, :], page[:])
